import numpy as np
import ml_dtypes


def mxq(x, axis, fmt="e4m3"):
    dtype, down = {"e4m3": (ml_dtypes.float8_e4m3fn, 7), "e5m2": (ml_dtypes.float8_e5m2, 14)}[fmt]
    v = np.moveaxis(np.asarray(x, np.float32).astype(ml_dtypes.bfloat16).astype(np.float64), axis, -1)
    blocks = v.reshape(v.shape[:-1] + (-1, 32))
    amax = np.abs(blocks).max(-1, keepdims=True)
    byte = np.maximum(np.where(amax > 0, np.frexp(amax)[1] - 1 + 127, 0) - down, 1)
    scale = np.exp2(byte - 127.0)
    codes = (blocks / scale).astype(np.float32).astype(dtype).astype(np.float64)
    return np.moveaxis((codes * scale).reshape(v.shape), -1, axis)


WIDE = False


def mx_kscale(k):
    if not WIDE:
        return np.ones(k)
    levels = np.array([10, -10, 5, -5, 0])
    if k % 512:
        return np.exp2(np.random.permutation(np.resize(levels, k // 32))).repeat(32)
    a = np.empty((k // 512, 16))
    for p in range(k // 512):
        a[p, :8] = np.random.permutation(np.resize(levels, 8))
        for g in range(8):
            far = levels[np.abs(levels - a[p, g]) >= 10]
            a[p, g + 8] = far[np.random.randint(len(far))]
    return np.exp2(a.ravel()).repeat(32)


def f64(x):
    return np.asarray(x).astype(np.float64)


def striped(idx):
    return np.tile(idx.reshape(-1, 16).T, (8, 1)).astype(np.uint16)


def unstriped(offs):
    return offs[:16].T.reshape(-1).astype(np.int64)


E2M1 = np.array([0.0, 0.5, 1.0, 1.5, 2.0, 3.0, 4.0, 6.0, -0.0, -0.5, -1.0, -1.5, -2.0, -3.0, -4.0, -6.0])


def pack_weight(w, fmt):
    k, n = w.shape
    w = f64(np.asarray(w, np.float32).astype(ml_dtypes.bfloat16)).reshape(k // 32, 32, n)
    amax = np.abs(w).max(1)
    if fmt == "e4m3":
        byte = np.frexp(amax)[1] - 1 + 127 - 7
    else:
        mant, ex = np.frexp(amax / 6.0)
        byte = np.where(mant > 0.5, ex, ex - 1) + 127
    byte = np.clip(np.where(amax > 0, byte, 1), 1, 254)
    scaled = (w * np.exp2(127.0 - byte)[:, None, :]).reshape(k, n).astype(np.float32)
    by_word = np.ascontiguousarray(scaled.reshape(k // 512, 128, 4, n).transpose(0, 1, 3, 2))
    if fmt == "e4m3":
        words = by_word.astype(ml_dtypes.float8_e4m3fn).view(np.uint8)
    else:
        c = by_word.astype(ml_dtypes.float4_e2m1fn).view(np.uint8) & 0xF
        words = (c[..., 0::2] | (c[..., 1::2] << 4)).reshape(k // 512, 128, 2 * n)
    return np.ascontiguousarray(words), np.ascontiguousarray(byte.astype(np.uint8).reshape(k // 512, 16, n))


def unpack_weight(words, scales, fmt):
    g, _, n = scales.shape
    words = np.ascontiguousarray(words).reshape(g, 128, n, -1)
    if fmt == "e4m3":
        vals = words.view(ml_dtypes.float8_e4m3fn).astype(np.float64)
    else:
        nib = np.empty((g, 128, n, 4), np.uint8)
        nib[..., 0::2] = words & 0xF
        nib[..., 1::2] = words >> 4
        vals = E2M1[nib]
    vals = vals * np.repeat(np.exp2(scales.astype(np.float64) - 127.0), 8, axis=1)[..., None]
    return vals.transpose(0, 1, 3, 2).reshape(g * 512, n)


def sigmoid(v):
    return 1.0 / (1.0 + np.exp(-np.maximum(v, -700.0)))


K, T, E, C, H, N = 512, 640, 15, 128, 512, 128
TOP = 3


def by_expert(wq, xq):
    return np.concatenate([wq[e].T @ xq[:, e * C:(e + 1) * C] for e in range(E)], axis=1)


def setup_inputs():
    n = np.random.standard_normal
    s = mx_kscale(K)[:, None]
    u = mx_kscale(H)
    deal = np.repeat(np.arange(E), C).reshape(TOP, T)[:, np.random.permutation(T)]
    deal = np.take_along_axis(deal, np.argsort(np.random.rand(TOP, T), axis=0), axis=0)
    for _ in range(8):
        s_, t_ = np.random.permutation(T).reshape(2, -1); r = np.random.randint(TOP, size=T // 2); x, y = deal[r, s_].copy(), deal[r, t_].copy()
        ok = ~((deal[:, s_] == y).any(0) | (deal[:, t_] == x).any(0)); deal[r[ok], s_[ok]] = y[ok]; deal[r[ok], t_[ok]] = x[ok]
    order = np.lexsort((np.random.rand(TOP * T), deal.reshape(-1)))
    slot_token = order % T; pos = np.empty(TOP * T, np.int64); pos[order] = np.arange(TOP * T); pos = pos.reshape(TOP, T)
    g = np.random.uniform(0.5, 1.5, (TOP, T)); g = g / g.sum(0)
    x = pack_weight(n((K, T)) * s, "e4m3")
    return {
        "x_words": x[0],
        "x_scales": x[1],
        "w1": (n((E + 1, K, H)) / np.sqrt(K) / s[None]).astype(np.float32),
        "w3": (n((E + 1, K, H)) / np.sqrt(K) / s[None] * u[None, None, :]).astype(np.float32),
        "w2": (n((E + 1, H, N)) / np.sqrt(H) / u[None, :, None]).astype(np.float32),
        "gate": np.stack([np.tile(r, (N, 1)) for r in g]).astype(np.float32),
        "offs": striped(slot_token),
        "pos1": striped(pos[0]),
        "pos2": striped(pos[1]),
        "pos3": striped(pos[2]),
    }


def reference(x_words, x_scales, w1, w3, w2, gate, offs, pos1, pos2, pos3):
    idx = unstriped(offs)
    w1q, w3q, w2q = mxq(f64(w1), 1, "e4m3"), mxq(f64(w3), 1, "e4m3"), mxq(f64(w2), 1, "e4m3")
    xs = unpack_weight(x_words, x_scales, "e4m3")
    hs = sigmoid(w1q[E].T @ xs) * (w3q[E].T @ xs)
    ys = w2q[E].T @ mxq(hs, 0, "e4m3")
    xq = unpack_weight(x_words, x_scales, "e4m3")[:, idx]
    h = sigmoid(by_expert(w1q, xq))
    h = h * by_expert(w3q, xq)
    y = by_expert(w2q, mxq(h, 0, "e4m3"))
    return ys + sum(f64(gate[r]) * y[:, unstriped(p)] for r, p in enumerate((pos1, pos2, pos3)))

@@ -1,0 +1,219 @@
+from contextlib import ExitStack
+
+import concourse.mybir as mybir
+
+K, T, E, C, H, N = 512, 640, 15, 128, 512, 128
+TOP = 3
+FLOPS = 2 * (E * C + T) * (2 * K * H + H * N)
+
+F32 = mybir.dt.float32
+BF16 = mybir.dt.bfloat16
+I32 = mybir.dt.int32
+U32 = mybir.dt.uint32
+U16 = mybir.dt.uint16
+U8 = mybir.dt.uint8
+FP8X4 = mybir.dt.float8_e4m3fn_x4
+MULT = mybir.AluOpType.mult
+ADD = mybir.AluOpType.add
+SIGMOID = mybir.ActivationFunctionType.Sigmoid
+
+P = 128
+PACK = 4
+LIST_ROWS = 16
+SHARED = E
+GATHER_EXPERTS = 3
+RING = 16
+GROUPS = ((0, 4), (4, 4), (8, 4), (12, 2), (14, 1))
+DEFERRED = 12
+
+
+def tile_moe_shr_glu_sigmoid_kernel(
+    tc, x_words, x_scales, w1, w3, w2, gate, offs, pos1, pos2, pos3, out
+):
+    nc = tc.nc
+    with ExitStack() as ctx:
+        keep = ctx.enter_context(tc.tile_pool(name="keep", bufs=1))
+        ring = ctx.enter_context(tc.tile_pool(name="ring", bufs=RING))
+        work = ctx.enter_context(tc.tile_pool(name="work", bufs=2))
+        psum = ctx.enter_context(tc.psum_pool(name="psum", bufs=1))
+
+        def load_first(w, e):
+            raw = ring.tile([P, PACK, H], F32, name="raw", tag="raw")
+            nc.sync.dma_start(out=raw[:], in_=w[e].rearrange("(p j) c -> p j c", j=PACK))
+            return raw
+
+        def load_second(e0, count):
+            raw = ring.tile([P, count, PACK, N], F32, name="raw", tag="raw")
+            nc.sync.dma_start(
+                out=raw[:].rearrange("p e j n -> p e (j n)"),
+                in_=w2[e0 : e0 + count].rearrange("e (p j) n -> p e (j n)", j=PACK),
+            )
+            return raw
+
+        def quantize(rounded, width, tag, bufs):
+            codes = work.tile([P, width], U32, name="codes", tag=tag + "_codes", bufs=bufs, align_bytes=64)
+            scales = work.tile([P, width], U8, name="scales", tag=tag + "_scales", bufs=bufs, align_bytes=64)
+            nc.vector.quantize_mx(out=codes[:].bitcast(FP8X4), scales=scales[:], in_=rounded[:])
+            return codes, scales
+
+        def round_first(copy, raw, tag):
+            rounded = work.tile([P, PACK * H], BF16, name="rounded", tag=tag, bufs=3, align_bytes=64)
+            copy(
+                out=rounded[:].rearrange("p (t m j) -> p m j t", t=PACK, j=PACK),
+                in_=raw[:].rearrange("p j (m t) -> p m j t", t=PACK),
+            )
+            return rounded
+
+        def round_second(raw, count):
+            rounded = work.tile([P, count * PACK * N], BF16, name="rounded", tag="w2_bf", align_bytes=64)
+            nc.scalar.copy(
+                out=rounded[:].rearrange("p (e c i j) -> p e c j i", e=count, i=4, j=PACK),
+                in_=raw[:].rearrange("p e j (c i) -> p e c j i", i=4),
+            )
+            return rounded
+
+        def product(acc, lhs, lhs_cols, rhs, rhs_cols):
+            nc.tensor.matmul_mx(
+                out=acc,
+                lhsT=lhs[0][:, lhs_cols].bitcast(FP8X4),
+                lhsT_scale=lhs[1][:, lhs_cols],
+                rhs=rhs[0][:, rhs_cols].bitcast(FP8X4),
+                rhs_scale=rhs[1][:, rhs_cols],
+                start=True,
+                stop=True,
+            )
+
+        def pre_activations(w1q, w3q, tokens, cols):
+            a1 = psum.tile([P, PACK, C], F32, name="a1", tag="a1", bufs=3)
+            a3 = psum.tile([P, PACK, C], F32, name="a3", tag="a3", bufs=3)
+            for acc, wq in ((a1, w1q), (a3, w3q)):
+                for t in range(PACK):
+                    product(acc[:, t, :], wq, slice(t * P, (t + 1) * P), tokens, cols)
+            return a1, a3
+
+        def gated(a1, a3, sig, h_out):
+            sig = sig.rearrange("p (s t) -> p s t", t=PACK)
+            nc.scalar.activation(out=sig, in_=a1[:].rearrange("p t s -> p s t"), func=SIGMOID)
+            nc.vector.tensor_tensor(
+                out=h_out.rearrange("p (s t) -> p s t", t=PACK),
+                in0=a3[:].rearrange("p t s -> p s t"),
+                in1=sig,
+                op=MULT,
+            )
+
+        def own_sig():
+            sig = work.tile([P, C * PACK], F32, name="sig", tag="sig", bufs=3)
+            return sig[:]
+
+        def first_layer(raw1, raw3):
+            r1 = round_first(nc.scalar.copy, raw1, "w1_bf")
+            r3 = round_first(nc.vector.tensor_copy, raw3, "w3_bf")
+            return quantize(r1, H, "w1", 3), quantize(r3, H, "w3", 3)
+
+        words = keep.tile([P, T], U32, name="words", align_bytes=64)
+        plane = keep.tile([P, T], U8, name="plane", align_bytes=64)
+        offs_sb = keep.tile([P, E * C // LIST_ROWS], U16, name="offs_sb")
+        nc.vector.memset(plane[:].bitcast(I32), 0)
+        raw1 = load_first(w1, SHARED)
+        nc.sync.dma_start(out=words[:].bitcast(I32), in_=x_words[0].rearrange("p t r -> p (t r)").bitcast(I32))
+        for q in range(4):
+            nc.sync.dma_start(
+                out=plane[:].bitcast(I32)[32 * q : 32 * q + 4, :],
+                in_=x_scales[0].bitcast(I32)[4 * q : 4 * q + 4, :],
+            )
+        nc.sync.dma_start(offs_sb[:], offs)
+        raw3 = load_first(w3, SHARED)
+        raw2 = load_second(SHARED, 1)
+
+        y_slots = keep.tile([P, E * C], F32, name="y_slots")
+        y_shared = keep.tile([P, T], F32, name="y_shared")
+
+        w1q, w3q = first_layer(raw1, raw3)
+        w2q = quantize(round_second(raw2, 1), N, "w2", 2)
+        for c0, blocks in ((0, 4), (4 * C, 1)):
+            h_bf = work.tile([P, blocks * C * PACK], BF16, name="h_bf", tag="h_bf", align_bytes=64)
+            for b in range(blocks):
+                a1, a3 = pre_activations(w1q, w3q, (words, plane), slice(c0 + b * C, c0 + (b + 1) * C))
+                gated(a1, a3, own_sig(), h_bf[:, b * C * PACK : (b + 1) * C * PACK])
+            hq = quantize(h_bf, blocks * C, "h", 2)
+            acc = psum.tile([P, blocks * C], F32, name="y_acc", tag="y_acc", bufs=2)
+            product(acc[:], w2q, slice(0, N), hq, slice(0, blocks * C))
+            nc.scalar.copy(out=y_shared[:, c0 : c0 + blocks * C], in_=acc[:])
+
+        gathered = {}
+
+        def gather(e0):
+            n = GATHER_EXPERTS * C
+            cut = offs_sb[:, e0 * C // LIST_ROWS : (e0 * C + n) // LIST_ROWS]
+            g_words = work.tile([P, n], U32, name="g_words", tag="g_words", align_bytes=64)
+            g_plane = work.tile([P, n], U8, name="g_plane", tag="g_plane", align_bytes=64)
+            nc.vector.tensor_copy(g_words[:], words[:].indirect(cut))
+            nc.vector.tensor_copy(g_plane[:], plane[:].indirect(cut))
+            gathered[e0] = (g_words, g_plane)
+
+        def second_layer(e0, count, hq):
+            w2q = quantize(round_second(load_second(e0, count), count), count * N, "w2", 2)
+            acc = psum.tile([P, count * C], F32, name="y_acc", tag="y_acc", bufs=2)
+            for i in range(count):
+                product(acc[:, i * C : (i + 1) * C], w2q, slice(i * N, (i + 1) * N), hq, slice(i * C, (i + 1) * C))
+            nc.scalar.copy(out=y_slots[:, e0 * C : (e0 + count) * C], in_=acc[:])
+
+        group_of = {}
+        for e0, count in GROUPS:
+            for e in range(e0, e0 + count):
+                group_of[e] = (e0, count)
+        h_tiles = {}
+        h_codes = {}
+        lists = []
+
+        def finish(e, accs, sig):
+            e0, count = group_of[e]
+            if e == e0:
+                h_tiles[e0] = work.tile([P, count * C * PACK], BF16, name="h_bf", tag="h_bf", align_bytes=64)
+            gated(accs[0], accs[1], sig, h_tiles[e0][:, (e - e0) * C * PACK : (e - e0 + 1) * C * PACK])
+            if e == e0 + count - 1:
+                h_codes[e0] = quantize(h_tiles[e0], count * C, "h", 2)
+                if e0 < DEFERRED:
+                    second_layer(e0, count, h_codes[e0])
+                    pos_sb = keep.tile([P, T // LIST_ROWS], U16, name=f"pos_sb{e0}")
+                    nc.sync.dma_start(pos_sb[:], (pos1, pos2, pos3)[len(lists)])
+                    lists.append(pos_sb)
+
+        pending = None
+        for e in range(E):
+            raw1, raw3 = load_first(w1, e), load_first(w3, e)
+            if e % GATHER_EXPERTS == 0:
+                gather(e)
+            w1q, w3q = first_layer(raw1, raw3)
+            place = e % GATHER_EXPERTS
+            accs = pre_activations(w1q, w3q, gathered[e - place], slice(place * C, (place + 1) * C))
+            if pending is not None:
+                finish(e - 1, pending, raw1[:, 0, :])
+            pending = accs
+        finish(E - 1, pending, own_sig())
+        for e0, count in GROUPS:
+            if e0 >= DEFERRED:
+                second_layer(e0, count, h_codes[e0])
+
+        gates = []
+        for r in range(TOP):
+            g = ring.tile([P, T], F32, name="raw", tag="raw")
+            nc.sync.dma_start(out=g[:], in_=gate[r])
+            gates.append(g)
+
+        half = T // 2
+        for c0 in (0, half):
+            cols = slice(c0, c0 + half)
+            terms = []
+            for r in range(TOP):
+                term = keep.tile([P, half], F32, name=f"term{r}_{c0}")
+                cut = lists[r][:, c0 // LIST_ROWS : (c0 + half) // LIST_ROWS]
+                nc.vector.tensor_tensor(term[:], y_slots[:].indirect(cut), gates[r][:, cols], MULT)
+                terms.append(term)
+            left = keep.tile([P, half], F32, name=f"left{c0}")
+            right = keep.tile([P, half], F32, name=f"right{c0}")
+            total = keep.tile([P, half], F32, name=f"total{c0}")
+            nc.vector.tensor_tensor(left[:], terms[0][:], y_shared[:, cols], ADD)
+            nc.vector.tensor_tensor(right[:], terms[1][:], terms[2][:], ADD)
+            nc.vector.tensor_tensor(total[:], left[:], right[:], ADD)
+            nc.sync.dma_start(out=out[:, cols], in_=total[:])

@@ -59,8 +59,8 @@ def tile_moe_shr_glu_sigmoid_kernel(
         def round_first(copy, raw, tag):
             rounded = work.tile([P, PACK * H], BF16, name="rounded", tag=tag, bufs=3, align_bytes=64)
             copy(
-                out=rounded[:].rearrange("p (t m j) -> p m j t", t=PACK, j=PACK),
-                in_=raw[:].rearrange("p j (m t) -> p m j t", t=PACK),
+                out=rounded[:].rearrange("p (t m u j) -> p m j t u", t=PACK, u=2, j=PACK),
+                in_=raw[:].rearrange("p j (m u t) -> p m j t u", u=2, t=PACK),
             )
             return rounded
 

@@ -22,7 +22,7 @@ PACK = 4
 LIST_ROWS = 16
 SHARED = E
 GATHER_EXPERTS = 3
-RING = 16
+RING = 8
 GROUPS = ((0, 4), (4, 4), (8, 4), (12, 2), (14, 1))
 DEFERRED = 12
 
@@ -37,10 +37,10 @@ def tile_moe_shr_glu_sigmoid_kernel(
         work = ctx.enter_context(tc.tile_pool(name="work", bufs=2))
         psum = ctx.enter_context(tc.psum_pool(name="psum", bufs=1))
 
-        def load_first(w, e):
-            raw = ring.tile([P, PACK, H], F32, name="raw", tag="raw")
-            nc.sync.dma_start(out=raw[:], in_=w[e].rearrange("(p j) c -> p j c", j=PACK))
-            return raw
+        def load_first(w, e0, count):
+            raw = ring.tile([P, count, PACK * H], F32, name="raw", tag="raw")
+            nc.sync.dma_start(out=raw[:], in_=w[e0 : e0 + count].rearrange("e (p j) c -> p e (j c)", j=PACK))
+            return [raw[:, i, :] for i in range(count)]
 
         def load_second(e0, count):
             raw = ring.tile([P, count, PACK, N], F32, name="raw", tag="raw")
@@ -60,7 +60,7 @@ def tile_moe_shr_glu_sigmoid_kernel(
             rounded = work.tile([P, PACK * H], BF16, name="rounded", tag=tag, bufs=3, align_bytes=64)
             copy(
                 out=rounded[:].rearrange("p (t m u j) -> p m j t u", t=PACK, u=2, j=PACK),
-                in_=raw[:].rearrange("p j (m u t) -> p m j t u", u=2, t=PACK),
+                in_=raw.rearrange("p (j m u t) -> p m j t u", j=PACK, u=2, t=PACK),
             )
             return rounded
 
@@ -114,7 +114,7 @@ def tile_moe_shr_glu_sigmoid_kernel(
         plane = keep.tile([P, T], U8, name="plane", align_bytes=64)
         offs_sb = keep.tile([P, E * C // LIST_ROWS], U16, name="offs_sb")
         nc.vector.memset(plane[:].bitcast(I32), 0)
-        raw1 = load_first(w1, SHARED)
+        raw1 = load_first(w1, SHARED, 1)[0]
         nc.sync.dma_start(out=words[:].bitcast(I32), in_=x_words[0].rearrange("p t r -> p (t r)").bitcast(I32))
         for q in range(4):
             nc.sync.dma_start(
@@ -122,7 +122,7 @@ def tile_moe_shr_glu_sigmoid_kernel(
                 in_=x_scales[0].bitcast(I32)[4 * q : 4 * q + 4, :],
             )
         nc.sync.dma_start(offs_sb[:], offs)
-        raw3 = load_first(w3, SHARED)
+        raw3 = load_first(w3, SHARED, 1)[0]
         raw2 = load_second(SHARED, 1)
 
         y_slots = keep.tile([P, E * C], F32, name="y_slots")
@@ -181,25 +181,25 @@ def tile_moe_shr_glu_sigmoid_kernel(
 
         pending = None
         for e in range(E):
-            raw1, raw3 = load_first(w1, e), load_first(w3, e)
+            count = 2 if e < DEFERRED else 1
+            if e % count == 0:
+                raws1, raws3 = load_first(w1, e, count), load_first(w3, e, count)
+            raw1, raw3 = raws1[e % count], raws3[e % count]
             if e % GATHER_EXPERTS == 0:
                 gather(e)
             w1q, w3q = first_layer(raw1, raw3)
             place = e % GATHER_EXPERTS
             accs = pre_activations(w1q, w3q, gathered[e - place], slice(place * C, (place + 1) * C))
             if pending is not None:
-                finish(e - 1, pending, raw1[:, 0, :])
+                finish(e - 1, pending, raw1[:, 0 : C * PACK])
             pending = accs
         finish(E - 1, pending, own_sig())
         for e0, count in GROUPS:
             if e0 >= DEFERRED:
                 second_layer(e0, count, h_codes[e0])
 
-        gates = []
-        for r in range(TOP):
-            g = ring.tile([P, T], F32, name="raw", tag="raw")
-            nc.sync.dma_start(out=g[:], in_=gate[r])
-            gates.append(g)
+        gates = ring.tile([P, TOP, T], F32, name="raw", tag="raw")
+        nc.sync.dma_start(out=gates[:], in_=gate.rearrange("r p t -> p r t"))
 
         half = T // 2
         for c0 in (0, half):
@@ -208,7 +208,7 @@ def tile_moe_shr_glu_sigmoid_kernel(
             for r in range(TOP):
                 term = keep.tile([P, half], F32, name=f"term{r}_{c0}")
                 cut = lists[r][:, c0 // LIST_ROWS : (c0 + half) // LIST_ROWS]
-                nc.vector.tensor_tensor(term[:], y_slots[:].indirect(cut), gates[r][:, cols], MULT)
+                nc.vector.tensor_tensor(term[:], y_slots[:].indirect(cut), gates[:, r, cols], MULT)
                 terms.append(term)
             left = keep.tile([P, half], F32, name=f"left{c0}")
             right = keep.tile([P, half], F32, name=f"right{c0}")

from contextlib import ExitStack

import concourse.mybir as mybir

K, T, E, C, H, N = 512, 640, 15, 128, 512, 128
TOP = 3
FLOPS = 2 * (E * C + T) * (2 * K * H + H * N)

F32 = mybir.dt.float32
BF16 = mybir.dt.bfloat16
I32 = mybir.dt.int32
U32 = mybir.dt.uint32
U16 = mybir.dt.uint16
U8 = mybir.dt.uint8
FP8X4 = mybir.dt.float8_e4m3fn_x4
MULT = mybir.AluOpType.mult
ADD = mybir.AluOpType.add
SIGMOID = mybir.ActivationFunctionType.Sigmoid

P = 128
PACK = 4
LIST_ROWS = 16
SHARED = E
GATHER_EXPERTS = 3
RING = 8
GROUPS = ((0, 4), (4, 4), (8, 4), (12, 2), (14, 1))
DEFERRED = 12


def tile_moe_shr_glu_sigmoid_kernel(
    tc, x_words, x_scales, w1, w3, w2, gate, offs, pos1, pos2, pos3, out
):
    nc = tc.nc
    with ExitStack() as ctx:
        keep = ctx.enter_context(tc.tile_pool(name="keep", bufs=1))
        ring = ctx.enter_context(tc.tile_pool(name="ring", bufs=RING))
        work = ctx.enter_context(tc.tile_pool(name="work", bufs=2))
        psum = ctx.enter_context(tc.psum_pool(name="psum", bufs=1))

        def load_first(w, e0, count):
            raw = ring.tile([P, count, PACK * H], F32, name="raw", tag="raw")
            nc.sync.dma_start(out=raw[:], in_=w[e0 : e0 + count].rearrange("e (p j) c -> p e (j c)", j=PACK))
            return [raw[:, i, :] for i in range(count)]

        def load_second(e0, count):
            raw = ring.tile([P, count, PACK, N], F32, name="raw", tag="raw")
            nc.sync.dma_start(
                out=raw[:].rearrange("p e j n -> p e (j n)"),
                in_=w2[e0 : e0 + count].rearrange("e (p j) n -> p e (j n)", j=PACK),
            )
            return raw

        def quantize(rounded, width, tag, bufs):
            codes = work.tile([P, width], U32, name="codes", tag=tag + "_codes", bufs=bufs, align_bytes=64)
            scales = work.tile([P, width], U8, name="scales", tag=tag + "_scales", bufs=bufs, align_bytes=64)
            nc.vector.quantize_mx(out=codes[:].bitcast(FP8X4), scales=scales[:], in_=rounded[:])
            return codes, scales

        def round_first(copy, raw, tag):
            rounded = work.tile([P, PACK * H], BF16, name="rounded", tag=tag, bufs=3, align_bytes=64)
            copy(
                out=rounded[:].rearrange("p (t m u j) -> p m j t u", t=PACK, u=2, j=PACK),
                in_=raw.rearrange("p (j m u t) -> p m j t u", j=PACK, u=2, t=PACK),
            )
            return rounded

        def round_second(raw, count):
            rounded = work.tile([P, count * PACK * N], BF16, name="rounded", tag="w2_bf", align_bytes=64)
            nc.scalar.copy(
                out=rounded[:].rearrange("p (e c i j) -> p e c j i", e=count, i=4, j=PACK),
                in_=raw[:].rearrange("p e j (c i) -> p e c j i", i=4),
            )
            return rounded

        def product(acc, lhs, lhs_cols, rhs, rhs_cols):
            nc.tensor.matmul_mx(
                out=acc,
                lhsT=lhs[0][:, lhs_cols].bitcast(FP8X4),
                lhsT_scale=lhs[1][:, lhs_cols],
                rhs=rhs[0][:, rhs_cols].bitcast(FP8X4),
                rhs_scale=rhs[1][:, rhs_cols],
                start=True,
                stop=True,
            )

        def pre_activations(w1q, w3q, tokens, cols):
            a1 = psum.tile([P, PACK, C], F32, name="a1", tag="a1", bufs=3)
            a3 = psum.tile([P, PACK, C], F32, name="a3", tag="a3", bufs=3)
            for acc, wq in ((a1, w1q), (a3, w3q)):
                for t in range(PACK):
                    product(acc[:, t, :], wq, slice(t * P, (t + 1) * P), tokens, cols)
            return a1, a3

        def gated(a1, a3, sig, h_out):
            sig = sig.rearrange("p (s t) -> p s t", t=PACK)
            nc.scalar.activation(out=sig, in_=a1[:].rearrange("p t s -> p s t"), func=SIGMOID)
            nc.vector.tensor_tensor(
                out=h_out.rearrange("p (s t) -> p s t", t=PACK),
                in0=a3[:].rearrange("p t s -> p s t"),
                in1=sig,
                op=MULT,
            )

        def own_sig():
            sig = work.tile([P, C * PACK], F32, name="sig", tag="sig", bufs=3)
            return sig[:]

        def first_layer(raw1, raw3):
            r1 = round_first(nc.scalar.copy, raw1, "w1_bf")
            r3 = round_first(nc.vector.tensor_copy, raw3, "w3_bf")
            return quantize(r1, H, "w1", 3), quantize(r3, H, "w3", 3)

        words = keep.tile([P, T], U32, name="words", align_bytes=64)
        plane = keep.tile([P, T], U8, name="plane", align_bytes=64)
        offs_sb = keep.tile([P, E * C // LIST_ROWS], U16, name="offs_sb")
        nc.vector.memset(plane[:].bitcast(I32), 0)
        raw1 = load_first(w1, SHARED, 1)[0]
        nc.sync.dma_start(out=words[:].bitcast(I32), in_=x_words[0].rearrange("p t r -> p (t r)").bitcast(I32))
        for q in range(4):
            nc.sync.dma_start(
                out=plane[:].bitcast(I32)[32 * q : 32 * q + 4, :],
                in_=x_scales[0].bitcast(I32)[4 * q : 4 * q + 4, :],
            )
        nc.sync.dma_start(offs_sb[:], offs)
        raw3 = load_first(w3, SHARED, 1)[0]
        raw2 = load_second(SHARED, 1)

        y_slots = keep.tile([P, E * C], F32, name="y_slots")
        y_shared = keep.tile([P, T], F32, name="y_shared")

        w1q, w3q = first_layer(raw1, raw3)
        w2q = quantize(round_second(raw2, 1), N, "w2", 2)
        for c0, blocks in ((0, 4), (4 * C, 1)):
            h_bf = work.tile([P, blocks * C * PACK], BF16, name="h_bf", tag="h_bf", align_bytes=64)
            for b in range(blocks):
                a1, a3 = pre_activations(w1q, w3q, (words, plane), slice(c0 + b * C, c0 + (b + 1) * C))
                gated(a1, a3, own_sig(), h_bf[:, b * C * PACK : (b + 1) * C * PACK])
            hq = quantize(h_bf, blocks * C, "h", 2)
            acc = psum.tile([P, blocks * C], F32, name="y_acc", tag="y_acc", bufs=2)
            product(acc[:], w2q, slice(0, N), hq, slice(0, blocks * C))
            nc.scalar.copy(out=y_shared[:, c0 : c0 + blocks * C], in_=acc[:])

        gathered = {}

        def gather(e0):
            n = GATHER_EXPERTS * C
            cut = offs_sb[:, e0 * C // LIST_ROWS : (e0 * C + n) // LIST_ROWS]
            g_words = work.tile([P, n], U32, name="g_words", tag="g_words", align_bytes=64)
            g_plane = work.tile([P, n], U8, name="g_plane", tag="g_plane", align_bytes=64)
            nc.vector.tensor_copy(g_words[:], words[:].indirect(cut))
            nc.vector.tensor_copy(g_plane[:], plane[:].indirect(cut))
            gathered[e0] = (g_words, g_plane)

        def second_layer(e0, count, hq):
            w2q = quantize(round_second(load_second(e0, count), count), count * N, "w2", 2)
            acc = psum.tile([P, count * C], F32, name="y_acc", tag="y_acc", bufs=2)
            for i in range(count):
                product(acc[:, i * C : (i + 1) * C], w2q, slice(i * N, (i + 1) * N), hq, slice(i * C, (i + 1) * C))
            nc.scalar.copy(out=y_slots[:, e0 * C : (e0 + count) * C], in_=acc[:])

        group_of = {}
        for e0, count in GROUPS:
            for e in range(e0, e0 + count):
                group_of[e] = (e0, count)
        h_tiles = {}
        h_codes = {}
        lists = []

        def finish(e, accs, sig):
            e0, count = group_of[e]
            if e == e0:
                h_tiles[e0] = work.tile([P, count * C * PACK], BF16, name="h_bf", tag="h_bf", align_bytes=64)
            gated(accs[0], accs[1], sig, h_tiles[e0][:, (e - e0) * C * PACK : (e - e0 + 1) * C * PACK])
            if e == e0 + count - 1:
                h_codes[e0] = quantize(h_tiles[e0], count * C, "h", 2)
                if e0 < DEFERRED:
                    second_layer(e0, count, h_codes[e0])
                    pos_sb = keep.tile([P, T // LIST_ROWS], U16, name=f"pos_sb{e0}")
                    nc.sync.dma_start(pos_sb[:], (pos1, pos2, pos3)[len(lists)])
                    lists.append(pos_sb)

        pending = None
        for e in range(E):
            count = 2 if e < DEFERRED else 1
            if e % count == 0:
                raws1, raws3 = load_first(w1, e, count), load_first(w3, e, count)
            raw1, raw3 = raws1[e % count], raws3[e % count]
            if e % GATHER_EXPERTS == 0:
                gather(e)
            w1q, w3q = first_layer(raw1, raw3)
            place = e % GATHER_EXPERTS
            accs = pre_activations(w1q, w3q, gathered[e - place], slice(place * C, (place + 1) * C))
            if pending is not None:
                finish(e - 1, pending, raw1[:, 0 : C * PACK])
            pending = accs
        finish(E - 1, pending, own_sig())
        for e0, count in GROUPS:
            if e0 >= DEFERRED:
                second_layer(e0, count, h_codes[e0])

        gates = ring.tile([P, TOP, T], F32, name="raw", tag="raw")
        nc.sync.dma_start(out=gates[:], in_=gate.rearrange("r p t -> p r t"))

        half = T // 2
        for c0 in (0, half):
            cols = slice(c0, c0 + half)
            terms = []
            for r in range(TOP):
                term = keep.tile([P, half], F32, name=f"term{r}_{c0}")
                cut = lists[r][:, c0 // LIST_ROWS : (c0 + half) // LIST_ROWS]
                nc.vector.tensor_tensor(term[:], y_slots[:].indirect(cut), gates[:, r, cols], MULT)
                terms.append(term)
            left = keep.tile([P, half], F32, name=f"left{c0}")
            right = keep.tile([P, half], F32, name=f"right{c0}")
            total = keep.tile([P, half], F32, name=f"total{c0}")
            nc.vector.tensor_tensor(left[:], terms[0][:], y_shared[:, cols], ADD)
            nc.vector.tensor_tensor(right[:], terms[1][:], terms[2][:], ADD)
            nc.vector.tensor_tensor(total[:], left[:], right[:], ADD)
            nc.sync.dma_start(out=out[:, cols], in_=total[:])
